import numpy as np
import ml_dtypes


def mxq(x, axis, fmt="e4m3"):
    dtype, down = {"e4m3": (ml_dtypes.float8_e4m3fn, 7), "e5m2": (ml_dtypes.float8_e5m2, 14)}[fmt]
    v = np.moveaxis(np.asarray(x, np.float32).astype(ml_dtypes.bfloat16).astype(np.float64), axis, -1)
    blocks = v.reshape(v.shape[:-1] + (-1, 32))
    amax = np.abs(blocks).max(-1, keepdims=True)
    byte = np.maximum(np.where(amax > 0, np.frexp(amax)[1] - 1 + 127, 0) - down, 1)
    scale = np.exp2(byte - 127.0)
    codes = (blocks / scale).astype(np.float32).astype(dtype).astype(np.float64)
    return np.moveaxis((codes * scale).reshape(v.shape), -1, axis)


WIDE = False


def mx_kscale(k):
    if not WIDE:
        return np.ones(k)
    levels = np.array([10, -10, 5, -5, 0])
    if k % 512:
        return np.exp2(np.random.permutation(np.resize(levels, k // 32))).repeat(32)
    a = np.empty((k // 512, 16))
    for p in range(k // 512):
        a[p, :8] = np.random.permutation(np.resize(levels, 8))
        for g in range(8):
            far = levels[np.abs(levels - a[p, g]) >= 10]
            a[p, g + 8] = far[np.random.randint(len(far))]
    return np.exp2(a.ravel()).repeat(32)


def f64(x):
    return np.asarray(x).astype(np.float64)


def striped(idx):
    return np.tile(idx.reshape(-1, 16).T, (8, 1)).astype(np.uint16)


def unstriped(offs):
    return offs[:16].T.reshape(-1).astype(np.int64)


def pack_weight(w):
    k, n = w.shape
    w = f64(np.asarray(w, np.float32).astype(ml_dtypes.bfloat16)).reshape(k // 32, 32, n)
    amax = np.abs(w).max(1)
    byte = np.clip(np.where(amax > 0, np.frexp(amax)[1] - 1 + 127 - 7, 1), 1, 254)
    scaled = (w * np.exp2(127.0 - byte)[:, None, :]).reshape(k, n).astype(np.float32)
    words = np.ascontiguousarray(scaled.reshape(k // 512, 128, 4, n).transpose(0, 1, 3, 2)).astype(ml_dtypes.float8_e4m3fn).view(np.uint8)
    return words, np.ascontiguousarray(byte.astype(np.uint8).reshape(k // 512, 16, n))


def unpack_weight(words, scales):
    g, p, n, _ = words.shape
    vals = np.ascontiguousarray(words).view(ml_dtypes.float8_e4m3fn).astype(np.float64) * np.repeat(np.exp2(scales.astype(np.float64) - 127.0), 8, axis=1)[..., None]
    return vals.transpose(0, 1, 3, 2).reshape(g * 512, n)


def silu(v):
    return v / (1.0 + np.exp(-np.maximum(v, -700.0)))


K, T, S, J, H, N = 1024, 2048, 768, 512, 512, 512


def setup_inputs():
    n = np.random.standard_normal
    s = mx_kscale(K)[:, None]
    u = mx_kscale(H)
    r = mx_kscale(J)[:, None]
    packed = pack_weight(n((K, T)) * s)
    return {
        "x_words": packed[0],
        "x_scales": packed[1],
        "eT": (n((J, S)) * r).astype(np.float32),
        "w1": (n((K, H)) / np.sqrt(K) / s * u).astype(np.float32),
        "w3": (n((J, H)) / np.sqrt(J) / r).astype(np.float32),
        "w2": (n((H, N)) / np.sqrt(H) / u[:, None]).astype(np.float32),
        "offs": striped(np.random.permutation(T)[:S]),
    }


def reference(x_words, x_scales, eT, w1, w3, w2, offs):
    c = mxq(f64(w1), 0, "e4m3").T @ unpack_weight(x_words, x_scales)[:, unstriped(offs)]
    z = c * silu(mxq(f64(w3), 0, "e4m3").T @ mxq(f64(eT), 0, "e4m3"))
    return mxq(f64(w2), 0, "e4m3").T @ mxq(z, 0, "e4m3")

@@ -1,0 +1,191 @@
+from contextlib import ExitStack
+
+import concourse.mybir as mybir
+
+K, T, S, J, H, N = 1024, 2048, 768, 512, 512, 512
+FLOPS = 2 * S * (K * H + J * H + H * N)
+
+F32 = mybir.dt.float32
+BF16 = mybir.dt.bfloat16
+I32 = mybir.dt.int32
+U32 = mybir.dt.uint32
+U16 = mybir.dt.uint16
+U8 = mybir.dt.uint8
+FP8X4 = mybir.dt.float8_e4m3fn_x4
+SILU = mybir.ActivationFunctionType.Silu
+MULT = mybir.AluOpType.mult
+
+P = 128
+PACK = 4
+K_PASS = P * PACK
+CHUNK = 256
+HALF = 128
+CHUNKS = S // CHUNK
+
+
+def tile_picked_schnet_silu_p_kernel(tc, x_words, x_scales, eT, w1, w3, w2, offs, out):
+    nc = tc.nc
+    with ExitStack() as ctx:
+        keep = ctx.enter_context(tc.tile_pool(name="keep", bufs=1))
+        psum = ctx.enter_context(tc.psum_pool(name="psum", bufs=1))
+
+        def copy_on(engine, dst, src):
+            if engine == "vector":
+                nc.vector.tensor_copy(out=dst, in_=src)
+            else:
+                nc.scalar.copy(out=dst, in_=src)
+
+        def load_rows(name, rows):
+            raw = keep.tile([P, PACK, rows.shape[1]], F32, name=name)
+            nc.sync.dma_start(out=raw[:], in_=rows.rearrange("(p j) w -> p j w", j=PACK))
+            return raw
+
+        def load_words(g):
+            table = keep.tile([P, T], U32, name="words%d" % g)
+            nc.sync.dma_start(out=table[:].bitcast(I32), in_=x_words[g].rearrange("p n t -> p (n t)").bitcast(I32))
+            return table
+
+        def round_plain(name, raw, shares):
+            width = raw.shape[2]
+            grouped = keep.tile([P, width * PACK], BF16, name=name, align_bytes=64)
+            dst = grouped[:].rearrange("p (c i j) -> p c j i", i=4, j=PACK)
+            src = raw[:].rearrange("p j (c i) -> p c j i", i=4)
+            for engine, lo, hi in shares:
+                copy_on(engine, dst[:, lo:hi], src[:, lo:hi])
+            return grouped
+
+        def round_dealt(name, raw, shares):
+            grouped = keep.tile([P, H * PACK], BF16, name=name, align_bytes=64)
+            dst = grouped[:].rearrange("p (t m j) -> p m j t", t=PACK, j=PACK)
+            src = raw[:].rearrange("p j (m t) -> p m j t", t=PACK)
+            for engine, lo, hi in shares:
+                copy_on(engine, dst[:, lo:hi], src[:, lo:hi])
+            return grouped
+
+        def quantize(name, grouped):
+            width = grouped.shape[1] // PACK
+            codes = keep.tile([P, width], U32, name=name + "_codes", align_bytes=64)
+            scales = keep.tile([P, width], U8, name=name + "_scales", align_bytes=64)
+            nc.vector.quantize_mx(out=codes[:].bitcast(FP8X4), scales=scales[:], in_=grouped[:])
+            return codes, scales
+
+        def product(acc, lhs, lhs_cols, rhs_codes, rhs_scales, start, stop):
+            nc.tensor.matmul_mx(
+                out=acc,
+                lhsT=lhs[0][:, lhs_cols].bitcast(FP8X4),
+                lhsT_scale=lhs[1][:, lhs_cols],
+                rhs=rhs_codes.bitcast(FP8X4),
+                rhs_scale=rhs_scales,
+                start=start,
+                stop=stop,
+            )
+
+        offsets = keep.tile([P, S // 16], U16, name="offsets")
+        nc.sync.dma_start(offsets[:], offs)
+        scale_table = keep.tile([P, T], U8, name="scale_table")
+        nc.vector.memset(scale_table[:].bitcast(I32), 0)
+        warm = keep.tile([P, 8], F32, name="warm")
+        nc.vector.memset(warm[:], 0.0)
+        warm2 = keep.tile([P, 8], F32, name="warm2")
+        nc.scalar.activation(out=warm2[:], in_=warm[:], func=SILU)
+        e0 = load_rows("e0", eT[:, 0:256])
+        for q in range(4):
+            nc.sync.dma_start(out=scale_table[32 * q : 32 * q + 8, :].bitcast(I32), in_=x_scales[:, 4 * q : 4 * q + 4, :].bitcast(I32))
+        w3r = load_rows("w3r", w3)
+        x0 = load_words(0)
+        w1a = load_rows("w1a", w1[0:512, :])
+        e1 = load_rows("e1", eT[:, 256:768])
+        w1b = load_rows("w1b", w1[512:1024, :])
+        x1 = load_words(1)
+        w2_0 = load_rows("w2_0", w2[:, 0:256])
+        w2_1 = load_rows("w2_1", w2[:, 256:512])
+
+        def gather(name, dtype, table, lo, n):
+            picked = keep.tile([P, n], dtype, name=name, align_bytes=64)
+            nc.vector.tensor_copy(picked[:], table[:].indirect(offsets[:, lo // 16 : (lo + n) // 16]))
+            return picked
+
+        def quantize_part(name, grouped, lo, n):
+            codes = keep.tile([P, n], U32, name=name + "_codes", align_bytes=64)
+            scales = keep.tile([P, n], U8, name=name + "_scales", align_bytes=64)
+            nc.vector.quantize_mx(out=codes[:].bitcast(FP8X4), scales=scales[:], in_=grouped[:, PACK * lo : PACK * (lo + n)])
+            return codes, scales
+
+        def edge_filter(u, e_mx, lo, tag):
+            bank = psum.tile([P, PACK, HALF], F32, name="f_bank%d" % u, tag=tag)
+            cols = slice(lo, lo + HALF)
+            for t in range(PACK):
+                product(bank[:, t, :], w3_mx, slice(t * P, (t + 1) * P), e_mx[0][:, cols], e_mx[1][:, cols], True, True)
+            gate = keep.tile([P, HALF, PACK], F32, name="gate%d" % u)
+            nc.scalar.activation(out=gate[:], in_=bank[:].rearrange("p t n -> p n t"), func=SILU)
+            return gate
+
+        def atom_product(u, words0, words1):
+            bank = psum.tile([P, PACK, HALF], F32, name="c_bank%d" % u, tag="c%d" % u)
+            cols = slice(u * HALF, (u + 1) * HALF)
+            for t in range(PACK):
+                lhs_cols = slice(t * P, (t + 1) * P)
+                product(bank[:, t, :], w1a_mx, lhs_cols, words0, picked_scales[:, cols], True, False)
+                product(bank[:, t, :], w1b_mx, lhs_cols, words1, picked_scales[4:, cols], False, True)
+            return bank
+
+        def message(z, lo, bank, gate):
+            zv = z[:].rearrange("p (n t) -> p n t", t=PACK)
+            nc.vector.tensor_tensor(out=zv[:, lo : lo + HALF, :], in0=bank[:].rearrange("p t n -> p n t"), in1=gate[:], op=MULT)
+
+        def project(name, lo, n, h, w_mx, w_lo, z_mx, tag, engine):
+            bank = psum.tile([P, 2, n], F32, name="o_bank" + name, tag=tag)
+            for u in range(2):
+                product(bank[:, u, :], w_mx, slice(w_lo + u * P, w_lo + (u + 1) * P), z_mx[0][:], z_mx[1][:], True, True)
+            staged = keep.tile([P, 2, n], F32, name="staged" + name)
+            copy_on(engine, staged[:], bank[:])
+            rows = out[2 * h * P : (2 * h + 2) * P, lo : lo + n]
+            nc.sync.dma_start(out=rows.rearrange("(u p) n -> p u n", u=2), in_=staged[:])
+
+        w2_0_mx = quantize("w2_0", round_plain("w2_0g", w2_0, [("scalar", 0, 64)]))
+        w2_1_mx = quantize("w2_1", round_plain("w2_1g", w2_1, [("scalar", 0, 64)]))
+        e0g = round_plain("e0g", e0, [("scalar", 0, 16), ("vector", 16, 64)])
+        e0q0 = quantize_part("e0q0", e0g, 0, 256)
+        picked_scales = gather("picked_scales", U8, scale_table, 0, S)
+        w3_mx = quantize("w3", round_dealt("w3g", w3r, [("scalar", 0, 64), ("vector", 64, 128)]))
+        gate0 = edge_filter(0, e0q0, 0, "f0")
+        gate1 = edge_filter(1, e0q0, 128, "f1")
+        g00 = gather("g00", U32, x0, 0, 768)
+        w1a_mx = quantize("w1a", round_dealt("w1ag", w1a, [("scalar", 0, 96), ("vector", 96, 128)]))
+        e1g = round_plain("e1g", e1, [("scalar", 0, 64), ("vector", 64, 128)])
+        e1q0 = quantize_part("e1q0", e1g, 0, 512)
+        gate2 = edge_filter(2, e1q0, 0, "f0")
+        gate3 = edge_filter(3, e1q0, 128, "f1")
+        gate4 = edge_filter(4, e1q0, 256, "f0")
+        gate5 = edge_filter(5, e1q0, 384, "f1")
+        w1b_mx = quantize("w1b", round_dealt("w1bg", w1b, [("scalar", 0, 64), ("vector", 64, 128)]))
+        g10 = gather("g10", U32, x1, 0, 256)
+        c0 = atom_product(0, g00[:, 0:128], g10[:, 0:128])
+        z0 = keep.tile([P, 1024], BF16, name="z0", align_bytes=64)
+        message(z0, 0, c0, gate0)
+        c1 = atom_product(1, g00[:, 128:256], g10[:, 128:256])
+        message(z0, 128, c1, gate1)
+        z0_mx = quantize("z0", z0)
+        project("00", 0, 256, 0, w2_0_mx, 0, z0_mx, "c0", "scalar")
+        project("01", 0, 256, 1, w2_1_mx, 0, z0_mx, "c1", "scalar")
+        g12 = gather("g12", U32, x1, 256, 512)
+        c2 = atom_product(2, g00[:, 256:384], g12[:, 0:128])
+        z1 = keep.tile([P, 1024], BF16, name="z1", align_bytes=64)
+        message(z1, 0, c2, gate2)
+        c3 = atom_product(3, g00[:, 384:512], g12[:, 128:256])
+        message(z1, 128, c3, gate3)
+        z1_mx = quantize("z1", z1)
+        project("10", 256, 256, 0, w2_0_mx, 0, z1_mx, "c2", "scalar")
+        project("11", 256, 256, 1, w2_1_mx, 0, z1_mx, "c3", "scalar")
+        c4 = atom_product(4, g00[:, 512:640], g12[:, 256:384])
+        z2 = keep.tile([P, 512], BF16, name="z2", align_bytes=64)
+        message(z2, 0, c4, gate4)
+        z2_mx = quantize("z2", z2)
+        project("20", 512, 128, 0, w2_0_mx, 0, z2_mx, "c4", "scalar")
+        project("21", 512, 128, 1, w2_1_mx, 0, z2_mx, "f1", "vector")
+        c5 = atom_product(5, g00[:, 640:768], g12[:, 384:512])
+        z3 = keep.tile([P, 512], BF16, name="z3", align_bytes=64)
+        message(z3, 0, c5, gate5)
+        z3_mx = quantize("z3", z3)
+        project("30", 640, 128, 0, w2_0_mx, 0, z3_mx, "c5", "scalar")
+        project("31", 640, 128, 1, w2_1_mx, 0, z3_mx, "f1", "vector")

@@ -49,7 +49,7 @@ def tile_picked_schnet_silu_p_kernel(tc, x_words, x_scales, eT, w1, w3, w2, offs
             width = raw.shape[2]
             grouped = keep.tile([P, width * PACK], BF16, name=name, align_bytes=64)
             dst = grouped[:].rearrange("p (c i j) -> p c j i", i=4, j=PACK)
-            src = raw[:].rearrange("p j (c i) -> p c j i", i=4)
+            src = raw[:, :, :].rearrange("p j (c i) -> p c j i", i=4)
             for engine, lo, hi in shares:
                 copy_on(engine, dst[:, lo:hi], src[:, lo:hi])
             return grouped
@@ -88,14 +88,13 @@ def tile_picked_schnet_silu_p_kernel(tc, x_words, x_scales, eT, w1, w3, w2, offs
         nc.vector.memset(warm[:], 0.0)
         warm2 = keep.tile([P, 8], F32, name="warm2")
         nc.scalar.activation(out=warm2[:], in_=warm[:], func=SILU)
-        e0 = load_rows("e0", eT[:, 0:256])
+        w3r = load_rows("w3r", w3)
         for q in range(4):
             nc.sync.dma_start(out=scale_table[32 * q : 32 * q + 8, :].bitcast(I32), in_=x_scales[:, 4 * q : 4 * q + 4, :].bitcast(I32))
-        w3r = load_rows("w3r", w3)
-        x0 = load_words(0)
         w1a = load_rows("w1a", w1[0:512, :])
-        e1 = load_rows("e1", eT[:, 256:768])
+        e0 = load_rows("e0", eT[:, 0:768])
         w1b = load_rows("w1b", w1[512:1024, :])
+        x0 = load_words(0)
         x1 = load_words(1)
         w2_0 = load_rows("w2_0", w2[:, 0:256])
         w2_1 = load_rows("w2_1", w2[:, 256:512])
@@ -144,22 +143,22 @@ def tile_picked_schnet_silu_p_kernel(tc, x_words, x_scales, eT, w1, w3, w2, offs
 
         w2_0_mx = quantize("w2_0", round_plain("w2_0g", w2_0, [("scalar", 0, 64)]))
         w2_1_mx = quantize("w2_1", round_plain("w2_1g", w2_1, [("scalar", 0, 64)]))
-        e0g = round_plain("e0g", e0, [("scalar", 0, 16), ("vector", 16, 64)])
-        e0q0 = quantize_part("e0q0", e0g, 0, 256)
-        picked_scales = gather("picked_scales", U8, scale_table, 0, S)
         w3_mx = quantize("w3", round_dealt("w3g", w3r, [("scalar", 0, 64), ("vector", 64, 128)]))
-        gate0 = edge_filter(0, e0q0, 0, "f0")
-        gate1 = edge_filter(1, e0q0, 128, "f1")
+        picked_scales = gather("picked_scales", U8, scale_table, 0, S)
+        w1a_mx = quantize("w1a", round_dealt("w1ag", w1a, [("scalar", 0, 128)]))
+        e0g = round_plain("e0g", e0, [("scalar", 0, 48), ("vector", 48, 192)])
+        e0q0 = quantize_part("e0q0", e0g, 0, 512)
+        e0q4 = quantize_part("e0q4", e0g, 512, 256)
+        gate0 = edge_filter(0, e0q0, 0, "c0")
+        gate1 = edge_filter(1, e0q0, 128, "c1")
+        gate2 = edge_filter(2, e0q0, 256, "c2")
+        gate3 = edge_filter(3, e0q0, 384, "c3")
+        gate4 = edge_filter(4, e0q4, 0, "c4")
+        gate5 = edge_filter(5, e0q4, 128, "c5")
+        w1b_mx = quantize("w1b", round_dealt("w1bg", w1b, [("vector", 0, 128)]))
         g00 = gather("g00", U32, x0, 0, 768)
-        w1a_mx = quantize("w1a", round_dealt("w1ag", w1a, [("scalar", 0, 96), ("vector", 96, 128)]))
-        e1g = round_plain("e1g", e1, [("scalar", 0, 64), ("vector", 64, 128)])
-        e1q0 = quantize_part("e1q0", e1g, 0, 512)
-        gate2 = edge_filter(2, e1q0, 0, "f0")
-        gate3 = edge_filter(3, e1q0, 128, "f1")
-        gate4 = edge_filter(4, e1q0, 256, "f0")
-        gate5 = edge_filter(5, e1q0, 384, "f1")
-        w1b_mx = quantize("w1b", round_dealt("w1bg", w1b, [("scalar", 0, 64), ("vector", 64, 128)]))
         g10 = gather("g10", U32, x1, 0, 256)
+        g12 = gather("g12", U32, x1, 256, 512)
         c0 = atom_product(0, g00[:, 0:128], g10[:, 0:128])
         z0 = keep.tile([P, 1024], BF16, name="z0", align_bytes=64)
         message(z0, 0, c0, gate0)
@@ -168,7 +167,6 @@ def tile_picked_schnet_silu_p_kernel(tc, x_words, x_scales, eT, w1, w3, w2, offs
         z0_mx = quantize("z0", z0)
         project("00", 0, 256, 0, w2_0_mx, 0, z0_mx, "c0", "scalar")
         project("01", 0, 256, 1, w2_1_mx, 0, z0_mx, "c1", "scalar")
-        g12 = gather("g12", U32, x1, 256, 512)
         c2 = atom_product(2, g00[:, 256:384], g12[:, 0:128])
         z1 = keep.tile([P, 1024], BF16, name="z1", align_bytes=64)
         message(z1, 0, c2, gate2)
@@ -182,10 +180,10 @@ def tile_picked_schnet_silu_p_kernel(tc, x_words, x_scales, eT, w1, w3, w2, offs
         message(z2, 0, c4, gate4)
         z2_mx = quantize("z2", z2)
         project("20", 512, 128, 0, w2_0_mx, 0, z2_mx, "c4", "scalar")
-        project("21", 512, 128, 1, w2_1_mx, 0, z2_mx, "f1", "vector")
+        project("21", 512, 128, 1, w2_1_mx, 0, z2_mx, "f0", "scalar")
         c5 = atom_product(5, g00[:, 640:768], g12[:, 384:512])
         z3 = keep.tile([P, 512], BF16, name="z3", align_bytes=64)
         message(z3, 0, c5, gate5)
         z3_mx = quantize("z3", z3)
-        project("30", 640, 128, 0, w2_0_mx, 0, z3_mx, "c5", "scalar")
-        project("31", 640, 128, 1, w2_1_mx, 0, z3_mx, "f1", "vector")
+        project("30", 640, 128, 0, w2_0_mx, 0, z3_mx, "c5", "vector")
+        project("31", 640, 128, 1, w2_1_mx, 0, z3_mx, "f1", "scalar")

from contextlib import ExitStack

import concourse.mybir as mybir

K, T, S, J, H, N = 1024, 2048, 768, 512, 512, 512
FLOPS = 2 * S * (K * H + J * H + H * N)

F32 = mybir.dt.float32
BF16 = mybir.dt.bfloat16
I32 = mybir.dt.int32
U32 = mybir.dt.uint32
U16 = mybir.dt.uint16
U8 = mybir.dt.uint8
FP8X4 = mybir.dt.float8_e4m3fn_x4
SILU = mybir.ActivationFunctionType.Silu
MULT = mybir.AluOpType.mult

P = 128
PACK = 4
K_PASS = P * PACK
CHUNK = 256
HALF = 128
CHUNKS = S // CHUNK


def tile_picked_schnet_silu_p_kernel(tc, x_words, x_scales, eT, w1, w3, w2, offs, out):
    nc = tc.nc
    with ExitStack() as ctx:
        keep = ctx.enter_context(tc.tile_pool(name="keep", bufs=1))
        psum = ctx.enter_context(tc.psum_pool(name="psum", bufs=1))

        def copy_on(engine, dst, src):
            if engine == "vector":
                nc.vector.tensor_copy(out=dst, in_=src)
            else:
                nc.scalar.copy(out=dst, in_=src)

        def load_rows(name, rows):
            raw = keep.tile([P, PACK, rows.shape[1]], F32, name=name)
            nc.sync.dma_start(out=raw[:], in_=rows.rearrange("(p j) w -> p j w", j=PACK))
            return raw

        def load_words(g):
            table = keep.tile([P, T], U32, name="words%d" % g)
            nc.sync.dma_start(out=table[:].bitcast(I32), in_=x_words[g].rearrange("p n t -> p (n t)").bitcast(I32))
            return table

        def round_plain(name, raw, shares):
            width = raw.shape[2]
            grouped = keep.tile([P, width * PACK], BF16, name=name, align_bytes=64)
            dst = grouped[:].rearrange("p (c i j) -> p c j i", i=4, j=PACK)
            src = raw[:, :, :].rearrange("p j (c i) -> p c j i", i=4)
            for engine, lo, hi in shares:
                copy_on(engine, dst[:, lo:hi], src[:, lo:hi])
            return grouped

        def round_dealt(name, raw, shares):
            grouped = keep.tile([P, H * PACK], BF16, name=name, align_bytes=64)
            dst = grouped[:].rearrange("p (t m j) -> p m j t", t=PACK, j=PACK)
            src = raw[:].rearrange("p j (m t) -> p m j t", t=PACK)
            for engine, lo, hi in shares:
                copy_on(engine, dst[:, lo:hi], src[:, lo:hi])
            return grouped

        def quantize(name, grouped):
            width = grouped.shape[1] // PACK
            codes = keep.tile([P, width], U32, name=name + "_codes", align_bytes=64)
            scales = keep.tile([P, width], U8, name=name + "_scales", align_bytes=64)
            nc.vector.quantize_mx(out=codes[:].bitcast(FP8X4), scales=scales[:], in_=grouped[:])
            return codes, scales

        def product(acc, lhs, lhs_cols, rhs_codes, rhs_scales, start, stop):
            nc.tensor.matmul_mx(
                out=acc,
                lhsT=lhs[0][:, lhs_cols].bitcast(FP8X4),
                lhsT_scale=lhs[1][:, lhs_cols],
                rhs=rhs_codes.bitcast(FP8X4),
                rhs_scale=rhs_scales,
                start=start,
                stop=stop,
            )

        offsets = keep.tile([P, S // 16], U16, name="offsets")
        nc.sync.dma_start(offsets[:], offs)
        scale_table = keep.tile([P, T], U8, name="scale_table")
        nc.vector.memset(scale_table[:].bitcast(I32), 0)
        warm = keep.tile([P, 8], F32, name="warm")
        nc.vector.memset(warm[:], 0.0)
        warm2 = keep.tile([P, 8], F32, name="warm2")
        nc.scalar.activation(out=warm2[:], in_=warm[:], func=SILU)
        w3r = load_rows("w3r", w3)
        for q in range(4):
            nc.sync.dma_start(out=scale_table[32 * q : 32 * q + 8, :].bitcast(I32), in_=x_scales[:, 4 * q : 4 * q + 4, :].bitcast(I32))
        w1a = load_rows("w1a", w1[0:512, :])
        e0 = load_rows("e0", eT[:, 0:768])
        w1b = load_rows("w1b", w1[512:1024, :])
        x0 = load_words(0)
        x1 = load_words(1)
        w2_0 = load_rows("w2_0", w2[:, 0:256])
        w2_1 = load_rows("w2_1", w2[:, 256:512])

        def gather(name, dtype, table, lo, n):
            picked = keep.tile([P, n], dtype, name=name, align_bytes=64)
            nc.vector.tensor_copy(picked[:], table[:].indirect(offsets[:, lo // 16 : (lo + n) // 16]))
            return picked

        def quantize_part(name, grouped, lo, n):
            codes = keep.tile([P, n], U32, name=name + "_codes", align_bytes=64)
            scales = keep.tile([P, n], U8, name=name + "_scales", align_bytes=64)
            nc.vector.quantize_mx(out=codes[:].bitcast(FP8X4), scales=scales[:], in_=grouped[:, PACK * lo : PACK * (lo + n)])
            return codes, scales

        def edge_filter(u, e_mx, lo, tag):
            bank = psum.tile([P, PACK, HALF], F32, name="f_bank%d" % u, tag=tag)
            cols = slice(lo, lo + HALF)
            for t in range(PACK):
                product(bank[:, t, :], w3_mx, slice(t * P, (t + 1) * P), e_mx[0][:, cols], e_mx[1][:, cols], True, True)
            gate = keep.tile([P, HALF, PACK], F32, name="gate%d" % u)
            nc.scalar.activation(out=gate[:], in_=bank[:].rearrange("p t n -> p n t"), func=SILU)
            return gate

        def atom_product(u, words0, words1):
            bank = psum.tile([P, PACK, HALF], F32, name="c_bank%d" % u, tag="c%d" % u)
            cols = slice(u * HALF, (u + 1) * HALF)
            for t in range(PACK):
                lhs_cols = slice(t * P, (t + 1) * P)
                product(bank[:, t, :], w1a_mx, lhs_cols, words0, picked_scales[:, cols], True, False)
                product(bank[:, t, :], w1b_mx, lhs_cols, words1, picked_scales[4:, cols], False, True)
            return bank

        def message(z, lo, bank, gate):
            zv = z[:].rearrange("p (n t) -> p n t", t=PACK)
            nc.vector.tensor_tensor(out=zv[:, lo : lo + HALF, :], in0=bank[:].rearrange("p t n -> p n t"), in1=gate[:], op=MULT)

        def project(name, lo, n, h, w_mx, w_lo, z_mx, tag, engine):
            bank = psum.tile([P, 2, n], F32, name="o_bank" + name, tag=tag)
            for u in range(2):
                product(bank[:, u, :], w_mx, slice(w_lo + u * P, w_lo + (u + 1) * P), z_mx[0][:], z_mx[1][:], True, True)
            staged = keep.tile([P, 2, n], F32, name="staged" + name)
            copy_on(engine, staged[:], bank[:])
            rows = out[2 * h * P : (2 * h + 2) * P, lo : lo + n]
            nc.sync.dma_start(out=rows.rearrange("(u p) n -> p u n", u=2), in_=staged[:])

        w2_0_mx = quantize("w2_0", round_plain("w2_0g", w2_0, [("scalar", 0, 64)]))
        w2_1_mx = quantize("w2_1", round_plain("w2_1g", w2_1, [("scalar", 0, 64)]))
        w3_mx = quantize("w3", round_dealt("w3g", w3r, [("scalar", 0, 64), ("vector", 64, 128)]))
        picked_scales = gather("picked_scales", U8, scale_table, 0, S)
        w1a_mx = quantize("w1a", round_dealt("w1ag", w1a, [("scalar", 0, 128)]))
        e0g = round_plain("e0g", e0, [("scalar", 0, 48), ("vector", 48, 192)])
        e0q0 = quantize_part("e0q0", e0g, 0, 512)
        e0q4 = quantize_part("e0q4", e0g, 512, 256)
        gate0 = edge_filter(0, e0q0, 0, "c0")
        gate1 = edge_filter(1, e0q0, 128, "c1")
        gate2 = edge_filter(2, e0q0, 256, "c2")
        gate3 = edge_filter(3, e0q0, 384, "c3")
        gate4 = edge_filter(4, e0q4, 0, "c4")
        gate5 = edge_filter(5, e0q4, 128, "c5")
        w1b_mx = quantize("w1b", round_dealt("w1bg", w1b, [("vector", 0, 128)]))
        g00 = gather("g00", U32, x0, 0, 768)
        g10 = gather("g10", U32, x1, 0, 256)
        g12 = gather("g12", U32, x1, 256, 512)
        c0 = atom_product(0, g00[:, 0:128], g10[:, 0:128])
        z0 = keep.tile([P, 1024], BF16, name="z0", align_bytes=64)
        message(z0, 0, c0, gate0)
        c1 = atom_product(1, g00[:, 128:256], g10[:, 128:256])
        message(z0, 128, c1, gate1)
        z0_mx = quantize("z0", z0)
        project("00", 0, 256, 0, w2_0_mx, 0, z0_mx, "c0", "scalar")
        project("01", 0, 256, 1, w2_1_mx, 0, z0_mx, "c1", "scalar")
        c2 = atom_product(2, g00[:, 256:384], g12[:, 0:128])
        z1 = keep.tile([P, 1024], BF16, name="z1", align_bytes=64)
        message(z1, 0, c2, gate2)
        c3 = atom_product(3, g00[:, 384:512], g12[:, 128:256])
        message(z1, 128, c3, gate3)
        z1_mx = quantize("z1", z1)
        project("10", 256, 256, 0, w2_0_mx, 0, z1_mx, "c2", "scalar")
        project("11", 256, 256, 1, w2_1_mx, 0, z1_mx, "c3", "scalar")
        c4 = atom_product(4, g00[:, 512:640], g12[:, 256:384])
        z2 = keep.tile([P, 512], BF16, name="z2", align_bytes=64)
        message(z2, 0, c4, gate4)
        z2_mx = quantize("z2", z2)
        project("20", 512, 128, 0, w2_0_mx, 0, z2_mx, "c4", "scalar")
        project("21", 512, 128, 1, w2_1_mx, 0, z2_mx, "f0", "scalar")
        c5 = atom_product(5, g00[:, 640:768], g12[:, 384:512])
        z3 = keep.tile([P, 512], BF16, name="z3", align_bytes=64)
        message(z3, 0, c5, gate5)
        z3_mx = quantize("z3", z3)
        project("30", 640, 128, 0, w2_0_mx, 0, z3_mx, "c5", "vector")
        project("31", 640, 128, 1, w2_1_mx, 0, z3_mx, "f1", "scalar")
